import numpy as np
import ml_dtypes


def mxq(x, axis, fmt="e4m3"):
    dtype, down = {"e4m3": (ml_dtypes.float8_e4m3fn, 7), "e5m2": (ml_dtypes.float8_e5m2, 14)}[fmt]
    v = np.moveaxis(np.asarray(x, np.float32).astype(ml_dtypes.bfloat16).astype(np.float64), axis, -1)
    blocks = v.reshape(v.shape[:-1] + (-1, 32))
    amax = np.abs(blocks).max(-1, keepdims=True)
    byte = np.maximum(np.where(amax > 0, np.frexp(amax)[1] - 1 + 127, 0) - down, 1)
    scale = np.exp2(byte - 127.0)
    codes = (blocks / scale).astype(np.float32).astype(dtype).astype(np.float64)
    return np.moveaxis((codes * scale).reshape(v.shape), -1, axis)


WIDE = False


def mx_kscale(k):
    if not WIDE:
        return np.ones(k)
    levels = np.array([30, -30])
    if k % 512:
        return np.exp2(np.random.permutation(np.resize(levels, k // 32))).repeat(32)
    a = np.empty((k // 512, 16))
    for p in range(k // 512):
        a[p, :8] = np.random.permutation(np.resize(levels, 8))
        for g in range(8):
            far = levels[np.abs(levels - a[p, g]) >= 10]
            a[p, g + 8] = far[np.random.randint(len(far))]
    return np.exp2(a.ravel()).repeat(32)


def f64(x):
    return np.asarray(x).astype(np.float64)


def striped(idx):
    return np.tile(np.asarray(idx).reshape(-1, 16).T, (8, 1)).astype(np.uint16)


def unstriped(offs):
    return offs[:16].T.reshape(-1).astype(np.int64)


E2M1 = np.array([0.0, 0.5, 1.0, 1.5, 2.0, 3.0, 4.0, 6.0, -0.0, -0.5, -1.0, -1.5, -2.0, -3.0, -4.0, -6.0])


def pack_weight(w, fmt):
    k, n = w.shape
    w = f64(np.asarray(w, np.float32).astype(ml_dtypes.bfloat16)).reshape(k // 32, 32, n)
    amax = np.abs(w).max(1)
    if fmt == "e4m3":
        byte = np.frexp(amax)[1] - 1 + 127 - 7
    else:
        mant, ex = np.frexp(amax / 6.0)
        byte = np.where(mant > 0.5, ex, ex - 1) + 127
    byte = np.clip(np.where(amax > 0, byte, 1), 1, 254)
    scaled = (w * np.exp2(127.0 - byte)[:, None, :]).reshape(k, n).astype(np.float32)
    by_word = np.ascontiguousarray(scaled.reshape(k // 512, 128, 4, n).transpose(0, 1, 3, 2))
    if fmt == "e4m3":
        words = by_word.astype(ml_dtypes.float8_e4m3fn).view(np.uint8)
    else:
        c = by_word.astype(ml_dtypes.float4_e2m1fn).view(np.uint8) & 0xF
        words = (c[..., 0::2] | (c[..., 1::2] << 4)).reshape(k // 512, 128, 2 * n)
    return np.ascontiguousarray(words), np.ascontiguousarray(byte.astype(np.uint8).reshape(k // 512, 16, n))


def unpack_weight(words, scales, fmt):
    g, _, n = scales.shape
    words = np.ascontiguousarray(words).reshape(g, 128, n, -1)
    if fmt == "e4m3":
        vals = words.view(ml_dtypes.float8_e4m3fn).astype(np.float64)
    else:
        nib = np.empty((g, 128, n, 4), np.uint8)
        nib[..., 0::2] = words & 0xF
        nib[..., 1::2] = words >> 4
        vals = E2M1[nib]
    vals = vals * np.repeat(np.exp2(scales.astype(np.float64) - 127.0), 8, axis=1)[..., None]
    return vals.transpose(0, 1, 3, 2).reshape(g * 512, n)


K, T, J, S, R, N = 512, 1024, 256, 512, 512, 256


def setup_inputs():
    n = np.random.standard_normal
    idx = np.random.permutation(T)[:J]
    idx2 = np.random.permutation(S)[:J]
    fk = mx_kscale(K)
    fr = mx_kscale(R)
    wbp = pack_weight(n((R, N)) * 1 / np.sqrt(R) / fr[:, None], "e2m1")
    return {
        "xa": (n((K, T))).astype(np.float32),
        "xb": (n((K, S))).astype(np.float32),
        "hb": (np.random.uniform(0.2, 0.9, (K, 1))).astype(np.float32),
        "fk": (np.random.uniform(0.5, 2.0, (K, 1)) / fk[:, None]).astype(np.float32),
        "w": (n((K, R)) * 1 / np.sqrt(K) * fk[:, None] * fr).astype(np.float32),
        "wb_words": wbp[0],
        "wb_scales": wbp[1],
        "rs": (1.0 * n((J, N))).astype(np.float32),
        "offs": striped(idx),
        "offs2": striped(idx2),
    }


def reference(xa, xb, hb, fk, w, wb_words, wb_scales, rs, offs, offs2):
    idx = unstriped(offs)
    idx2 = unstriped(offs2)
    wbu = unpack_weight(wb_words, wb_scales, "e2m1")
    u = (f64(xa)[:, idx] - np.minimum(f64(xb)[:, idx2], f64(hb))) * f64(fk)
    wq = mxq(f64(w), 0, "e5m2")
    uq = mxq(u, 0, "e4m3")
    a = wq.T @ uq
    ha = np.maximum(a, 0.0)
    h1 = np.pad(ha, ((0, 0), (2, 0)))[:, :J]
    hid = ha - 0.5 * h1
    hidq = mxq(hid, 0, "e5m2")
    p = hidq.T @ wbu
    mn = np.mean(np.abs(p), axis=1, keepdims=True)
    y = np.maximum(p - mn, 0.0) - 0.3 * f64(rs)
    return y

@@ -1,0 +1,158 @@
+from contextlib import ExitStack
+
+import concourse.mybir as mybir
+
+K, T, J, S, R, N = 512, 1024, 256, 512, 512, 256
+FLOPS = 2 * K * R * J + 2 * R * J * N
+
+F32 = mybir.dt.float32
+BF16 = mybir.dt.bfloat16
+I32 = mybir.dt.int32
+U32 = mybir.dt.uint32
+U16 = mybir.dt.uint16
+U8 = mybir.dt.uint8
+E4M3 = mybir.dt.float8_e4m3fn_x4
+E5M2 = mybir.dt.float8_e5m2_x4
+E2M1 = mybir.dt.float4_e2m1fn_x4
+ALU = mybir.AluOpType
+ACT = mybir.ActivationFunctionType
+
+P = 128
+PACK = 4
+HALF = J // 2
+QUARTER = J // 4
+LAG = 2
+W_SPLIT = 96
+
+
+def tile_list_boundedgaps_lagged_rowabove_kernel(tc, xa, xb, hb, fk, w, wb_words, wb_scales, rs, offs, offs2, out):
+    nc = tc.nc
+    with ExitStack() as ctx:
+        keep = ctx.enter_context(tc.tile_pool(name="keep", bufs=1))
+        psum = ctx.enter_context(tc.psum_pool(name="psum", bufs=1))
+
+        def sbuf(name, shape, dtype):
+            return keep.tile(shape, dtype, name=name, align_bytes=64)
+
+        list_a = sbuf("list_a", [P, J // 16], U16)
+        list_b = sbuf("list_b", [P, J // 16], U16)
+        w_raw = sbuf("w_raw", [P, PACK, R], F32)
+        bound = sbuf("bound", [P, PACK], F32)
+        factor = sbuf("factor", [P, PACK], F32)
+        xb_pairs = [sbuf(f"xb_pair{i}", [P, 2, S], F32) for i in range(2)]
+        xa_rows = [sbuf(f"xa_row{t}", [P, T], F32) for t in range(PACK)]
+        wb_codes = sbuf("wb_codes", [P, 2 * N], U8)
+        wb_scale = sbuf("wb_scale", [P, N], U8)
+        resid = sbuf("resid", [P, 2, N], F32)
+        relu_a = sbuf("relu_a", [P, PACK * (LAG + J)], F32)
+
+        nc.gpsimd.memset(wb_scale[:].bitcast(I32), 0)
+        nc.gpsimd.memset(relu_a[:, 0 : PACK * LAG], 0.0)
+
+        xa_v = xa.rearrange("(p t) c -> p t c", t=PACK)
+        xb_v = xb.rearrange("(p t) c -> p t c", t=PACK)
+        nc.sync.dma_start(w_raw[:], w.rearrange("(p t) r -> p t r", t=PACK))
+        nc.sync.dma_start(list_b[:], offs2)
+        nc.sync.dma_start(bound[:], hb.rearrange("(p t) o -> p (t o)", t=PACK))
+        for i in range(2):
+            nc.sync.dma_start(xb_pairs[i][:], xb_v[:, 2 * i : 2 * i + 2, :])
+        nc.sync.dma_start(list_a[:], offs)
+        nc.sync.dma_start(factor[:], fk.rearrange("(p t) o -> p (t o)", t=PACK))
+        for t in range(PACK):
+            nc.sync.dma_start(xa_rows[t][:], xa_v[:, t, :])
+        nc.sync.dma_start(wb_codes[:], wb_words[0])
+        for q in range(4):
+            nc.sync.dma_start(wb_scale[32 * q : 32 * q + 4, :].bitcast(I32), wb_scales[0, 4 * q : 4 * q + 4, :].bitcast(I32))
+        nc.sync.dma_start(resid[:], rs.rearrange("(h p) n -> p h n", p=P))
+
+        w_bf = sbuf("w_bf", [P, PACK * R], BF16)
+        w_dst = w_bf[:].rearrange("p (s m t) -> p m t s", s=PACK, t=PACK)
+        w_src = w_raw[:].rearrange("p t (m s) -> p m t s", s=PACK)
+        nc.vector.tensor_copy(w_dst[:, 0:W_SPLIT], w_src[:, 0:W_SPLIT])
+        nc.scalar.copy(w_dst[:, W_SPLIT:P], w_src[:, W_SPLIT:P])
+        w_codes = sbuf("w_codes", [P, R], U32)
+        w_scale = sbuf("w_scale", [P, R], U8)
+        nc.vector.quantize_mx(w_codes[:].bitcast(E5M2), w_scale[:], w_bf[:])
+
+        capped = []
+        for t in range(PACK):
+            picked_b = sbuf(f"picked_b{t}", [P, J], F32)
+            window = xb_pairs[t // 2][:, t % 2, :].indirect(list_b[:])
+            if t < 2:
+                nc.vector.tensor_copy(picked_b[:], window)
+            else:
+                nc.scalar.activation(picked_b[:], window, ACT.Copy)
+            cap = sbuf(f"capped{t}", [P, J], F32)
+            nc.vector.tensor_scalar(cap[:], picked_b[:], bound[:, t : t + 1], None, ALU.min)
+            capped.append(cap)
+
+        u_bf = [sbuf(f"u_bf{h}", [P, HALF, PACK], BF16) for h in range(2)]
+        halves = [slice(h * HALF, (h + 1) * HALF) for h in range(2)]
+        for t in range(PACK - 1):
+            gap = sbuf(f"gap{t}", [P, J], F32)
+            nc.vector.tensor_tensor(gap[:], xa_rows[t][:].indirect(list_a[:]), capped[t][:], ALU.subtract)
+            for h in range(2):
+                if t < 2:
+                    nc.scalar.activation(u_bf[h][:, :, t], gap[:, halves[h]], ACT.Copy, scale=factor[:, t : t + 1])
+                else:
+                    nc.vector.tensor_scalar(u_bf[h][:, :, t], gap[:, halves[h]], factor[:, t : t + 1], None, ALU.mult)
+        last = PACK - 1
+        cols = HALF // 16
+        a_banks = []
+        for h in range(2):
+            gap = sbuf(f"gap_last{h}", [P, HALF], F32)
+            nc.vector.tensor_tensor(
+                gap[:], xa_rows[last][:].indirect(list_a[:, h * cols : (h + 1) * cols]), capped[last][:, halves[h]], ALU.subtract
+            )
+            nc.vector.tensor_scalar(u_bf[h][:, :, last], gap[:], factor[:, last : last + 1], None, ALU.mult)
+            u_codes = sbuf(f"u_codes{h}", [P, HALF], U32)
+            u_scale = sbuf(f"u_scale{h}", [P, HALF], U8)
+            nc.vector.quantize_mx(u_codes[:].bitcast(E4M3), u_scale[:], u_bf[h][:].rearrange("p j t -> p (j t)"))
+            bank = psum.tile([P, PACK, HALF], F32, name=f"a_bank{h}")
+            for s in range(PACK):
+                nc.tensor.matmul_mx(
+                    out=bank[:, s, :],
+                    lhsT=w_codes[:, s * P : (s + 1) * P].bitcast(E5M2),
+                    lhsT_scale=w_scale[:, s * P : (s + 1) * P],
+                    rhs=u_codes[:].bitcast(E4M3),
+                    rhs_scale=u_scale[:],
+                    start=True,
+                    stop=True,
+                )
+            a_banks.append(bank)
+
+        width = PACK * QUARTER
+        for h in range(2):
+            hid_bf = sbuf(f"hid_bf{h}", [P, PACK * HALF], BF16)
+            for i in range(2):
+                lo = (2 * h + i) * width
+                now = relu_a[:, PACK * LAG + lo : PACK * LAG + lo + width]
+                nc.scalar.activation(
+                    now.rearrange("p (j s) -> p j s", s=PACK),
+                    a_banks[h][:, :, i * QUARTER : (i + 1) * QUARTER].rearrange("p s j -> p j s"),
+                    ACT.Relu,
+                )
+                nc.vector.scalar_tensor_tensor(
+                    hid_bf[:, i * width : (i + 1) * width], relu_a[:, lo : lo + width], -0.5, now, ALU.mult, ALU.add
+                )
+            hid_codes = sbuf(f"hid_codes{h}", [P, HALF], U32)
+            hid_scale = sbuf(f"hid_scale{h}", [P, HALF], U8)
+            nc.vector.quantize_mx(hid_codes[:].bitcast(E5M2), hid_scale[:], hid_bf[:])
+            prod = psum.tile([P, N], F32, name=f"p_bank{h}")
+            nc.tensor.matmul_mx(
+                out=prod[:],
+                lhsT=hid_codes[:].bitcast(E5M2),
+                lhsT_scale=hid_scale[:],
+                rhs=wb_codes[:].bitcast(E2M1),
+                rhs_scale=wb_scale[:],
+                start=True,
+                stop=True,
+            )
+            magnitude = sbuf(f"magnitude{h}", [P, N], F32)
+            mean = sbuf(f"mean{h}", [P, 1], F32)
+            nc.scalar.activation(magnitude[:], prod[:], ACT.Abs, scale=1.0 / N, accum_out=mean[:])
+            off = sbuf(f"off{h}", [P, N], F32)
+            y = sbuf(f"y{h}", [P, N], F32)
+            nc.vector.tensor_scalar(off[:], resid[:, h, :], 0.3, mean[:], ALU.mult, ALU.add)
+            nc.vector.scalar_tensor_tensor(y[:], prod[:], mean[:], off[:], ALU.max, ALU.subtract)
+            nc.sync.dma_start(out[halves[h], :], y[:])

@@ -22,7 +22,9 @@ PACK = 4
 HALF = J // 2
 QUARTER = J // 4
 LAG = 2
-W_SPLIT = 96
+W_SPLIT = 64
+ROW_ORDER = (2, 0, 1, 3)
+HID_PIECES = ((32, 32, 64), (64, 64))
 
 
 def tile_list_boundedgaps_lagged_rowabove_kernel(tc, xa, xb, hb, fk, w, wb_words, wb_scales, rs, offs, offs2, out):
@@ -46,25 +48,41 @@ def tile_list_boundedgaps_lagged_rowabove_kernel(tc, xa, xb, hb, fk, w, wb_words
         resid = sbuf("resid", [P, 2, N], F32)
         relu_a = sbuf("relu_a", [P, PACK * (LAG + J)], F32)
 
+        taken_off = sbuf("taken_off", [P, N], F32)
+
         nc.gpsimd.memset(wb_scale[:].bitcast(I32), 0)
         nc.gpsimd.memset(relu_a[:, 0 : PACK * LAG], 0.0)
 
         xa_v = xa.rearrange("(p t) c -> p t c", t=PACK)
         xb_v = xb.rearrange("(p t) c -> p t c", t=PACK)
-        nc.sync.dma_start(w_raw[:], w.rearrange("(p t) r -> p t r", t=PACK))
+        nc.scalar.dma_start(bound[:], hb.rearrange("(p t) o -> p (t o)", t=PACK))
+        nc.scalar.dma_start(factor[:], fk.rearrange("(p t) o -> p (t o)", t=PACK))
+        nc.sync.dma_start(xb_pairs[1][:], xb_v[:, 2:4, :])
         nc.sync.dma_start(list_b[:], offs2)
-        nc.sync.dma_start(bound[:], hb.rearrange("(p t) o -> p (t o)", t=PACK))
-        for i in range(2):
-            nc.sync.dma_start(xb_pairs[i][:], xb_v[:, 2 * i : 2 * i + 2, :])
+        nc.sync.dma_start(w_raw[:], w.rearrange("(p t) r -> p t r", t=PACK))
+        nc.sync.dma_start(xb_pairs[0][:], xb_v[:, 0:2, :])
         nc.sync.dma_start(list_a[:], offs)
-        nc.sync.dma_start(factor[:], fk.rearrange("(p t) o -> p (t o)", t=PACK))
-        for t in range(PACK):
+        for t in ROW_ORDER:
             nc.sync.dma_start(xa_rows[t][:], xa_v[:, t, :])
         nc.sync.dma_start(wb_codes[:], wb_words[0])
         for q in range(4):
             nc.sync.dma_start(wb_scale[32 * q : 32 * q + 4, :].bitcast(I32), wb_scales[0, 4 * q : 4 * q + 4, :].bitcast(I32))
         nc.sync.dma_start(resid[:], rs.rearrange("(h p) n -> p h n", p=P))
 
+        capped = {}
+
+        def cap_row(t):
+            picked_b = sbuf(f"picked_b{t}", [P, J], F32)
+            window = xb_pairs[t // 2][:, t % 2, :].indirect(list_b[:])
+            if t >= 2:
+                nc.vector.tensor_copy(picked_b[:], window)
+            else:
+                nc.scalar.activation(picked_b[:], window, ACT.Copy)
+            capped[t] = sbuf(f"capped{t}", [P, J], F32)
+            nc.vector.tensor_scalar(capped[t][:], picked_b[:], bound[:, t : t + 1], None, ALU.min)
+
+        cap_row(2)
+        cap_row(3)
         w_bf = sbuf("w_bf", [P, PACK * R], BF16)
         w_dst = w_bf[:].rearrange("p (s m t) -> p m t s", s=PACK, t=PACK)
         w_src = w_raw[:].rearrange("p t (m s) -> p m t s", s=PACK)
@@ -74,37 +92,33 @@ def tile_list_boundedgaps_lagged_rowabove_kernel(tc, xa, xb, hb, fk, w, wb_words
         w_scale = sbuf("w_scale", [P, R], U8)
         nc.vector.quantize_mx(w_codes[:].bitcast(E5M2), w_scale[:], w_bf[:])
 
-        capped = []
-        for t in range(PACK):
-            picked_b = sbuf(f"picked_b{t}", [P, J], F32)
-            window = xb_pairs[t // 2][:, t % 2, :].indirect(list_b[:])
-            if t < 2:
-                nc.vector.tensor_copy(picked_b[:], window)
-            else:
-                nc.scalar.activation(picked_b[:], window, ACT.Copy)
-            cap = sbuf(f"capped{t}", [P, J], F32)
-            nc.vector.tensor_scalar(cap[:], picked_b[:], bound[:, t : t + 1], None, ALU.min)
-            capped.append(cap)
+        cap_row(0)
+        cap_row(1)
 
         u_bf = [sbuf(f"u_bf{h}", [P, HALF, PACK], BF16) for h in range(2)]
         halves = [slice(h * HALF, (h + 1) * HALF) for h in range(2)]
-        for t in range(PACK - 1):
-            gap = sbuf(f"gap{t}", [P, J], F32)
-            nc.vector.tensor_tensor(gap[:], xa_rows[t][:].indirect(list_a[:]), capped[t][:], ALU.subtract)
-            for h in range(2):
-                if t < 2:
-                    nc.scalar.activation(u_bf[h][:, :, t], gap[:, halves[h]], ACT.Copy, scale=factor[:, t : t + 1])
-                else:
-                    nc.vector.tensor_scalar(u_bf[h][:, :, t], gap[:, halves[h]], factor[:, t : t + 1], None, ALU.mult)
-        last = PACK - 1
-        cols = HALF // 16
+
+        def scale_into(on_scalar, dst, src, t):
+            if on_scalar:
+                nc.scalar.activation(dst, src, ACT.Copy, scale=factor[:, t : t + 1])
+            else:
+                nc.vector.tensor_scalar(dst, src, factor[:, t : t + 1], None, ALU.mult)
+
+        pieces = {2: ((0, J),), 0: ((0, J),), 1: ((0, HALF), (HALF, HALF)), 3: ((0, QUARTER), (QUARTER, QUARTER), (HALF, HALF))}
+        for t in ROW_ORDER:
+            gaps = []
+            for lo, n in pieces[t]:
+                gap = sbuf(f"gap{t}_{lo}", [P, n], F32)
+                nc.vector.tensor_tensor(
+                    gap[:], xa_rows[t][:].indirect(list_a[:, lo // 16 : (lo + n) // 16]), capped[t][:, lo : lo + n], ALU.subtract
+                )
+                gaps.append((gap, lo, n))
+            for gap, lo, n in gaps:
+                for j in range(lo, lo + n, HALF):
+                    h, m = j // HALF, min(n, HALF)
+                    scale_into(t >= 2 or h == 1, u_bf[h][:, j % HALF : j % HALF + m, t], gap[:, j - lo : j - lo + m], t)
         a_banks = []
         for h in range(2):
-            gap = sbuf(f"gap_last{h}", [P, HALF], F32)
-            nc.vector.tensor_tensor(
-                gap[:], xa_rows[last][:].indirect(list_a[:, h * cols : (h + 1) * cols]), capped[last][:, halves[h]], ALU.subtract
-            )
-            nc.vector.tensor_scalar(u_bf[h][:, :, last], gap[:], factor[:, last : last + 1], None, ALU.mult)
             u_codes = sbuf(f"u_codes{h}", [P, HALF], U32)
             u_scale = sbuf(f"u_scale{h}", [P, HALF], U8)
             nc.vector.quantize_mx(u_codes[:].bitcast(E4M3), u_scale[:], u_bf[h][:].rearrange("p j t -> p (j t)"))
@@ -121,20 +135,21 @@ def tile_list_boundedgaps_lagged_rowabove_kernel(tc, xa, xb, hb, fk, w, wb_words
                 )
             a_banks.append(bank)
 
-        width = PACK * QUARTER
         for h in range(2):
             hid_bf = sbuf(f"hid_bf{h}", [P, PACK * HALF], BF16)
-            for i in range(2):
-                lo = (2 * h + i) * width
+            j0 = 0
+            for n in HID_PIECES[h]:
+                lo, width = PACK * (h * HALF + j0), PACK * n
                 now = relu_a[:, PACK * LAG + lo : PACK * LAG + lo + width]
                 nc.scalar.activation(
                     now.rearrange("p (j s) -> p j s", s=PACK),
-                    a_banks[h][:, :, i * QUARTER : (i + 1) * QUARTER].rearrange("p s j -> p j s"),
+                    a_banks[h][:, :, j0 : j0 + n].rearrange("p s j -> p j s"),
                     ACT.Relu,
                 )
                 nc.vector.scalar_tensor_tensor(
-                    hid_bf[:, i * width : (i + 1) * width], relu_a[:, lo : lo + width], -0.5, now, ALU.mult, ALU.add
+                    hid_bf[:, PACK * j0 : PACK * j0 + width], relu_a[:, lo : lo + width], -0.5, now, ALU.mult, ALU.add
                 )
+                j0 = j0 + n
             hid_codes = sbuf(f"hid_codes{h}", [P, HALF], U32)
             hid_scale = sbuf(f"hid_scale{h}", [P, HALF], U8)
             nc.vector.quantize_mx(hid_codes[:].bitcast(E5M2), hid_scale[:], hid_bf[:])
@@ -151,8 +166,14 @@ def tile_list_boundedgaps_lagged_rowabove_kernel(tc, xa, xb, hb, fk, w, wb_words
             magnitude = sbuf(f"magnitude{h}", [P, N], F32)
             mean = sbuf(f"mean{h}", [P, 1], F32)
             nc.scalar.activation(magnitude[:], prod[:], ACT.Abs, scale=1.0 / N, accum_out=mean[:])
-            off = sbuf(f"off{h}", [P, N], F32)
-            y = sbuf(f"y{h}", [P, N], F32)
-            nc.vector.tensor_scalar(off[:], resid[:, h, :], 0.3, mean[:], ALU.mult, ALU.add)
-            nc.vector.scalar_tensor_tensor(y[:], prod[:], mean[:], off[:], ALU.max, ALU.subtract)
-            nc.sync.dma_start(out[halves[h], :], y[:])
+            parts = 1 + h
+            part = N // parts
+            offsets_n = [slice(c * part, (c + 1) * part) for c in range(parts)]
+            off = [taken_off[:, offsets_n[c]] for c in range(parts)]
+            y = [sbuf(f"y{h}_{c}", [P, part], F32) for c in range(parts)]
+            for c in range(parts):
+                nc.vector.tensor_scalar(off[c], resid[:, h, offsets_n[c]], 0.3, mean[:], ALU.mult, ALU.add)
+            for c in range(parts):
+                nc.vector.scalar_tensor_tensor(y[c][:], prod[:, offsets_n[c]], mean[:], off[c], ALU.max, ALU.subtract)
+                queue = nc.sync if c == parts - 1 else nc.scalar
+                queue.dma_start(out[halves[h], offsets_n[c]], y[c][:])

@@ -22,7 +22,7 @@ PACK = 4
 HALF = J // 2
 QUARTER = J // 4
 LAG = 2
-W_SPLIT = 64
+W_SPLIT = 80
 ROW_ORDER = (2, 0, 1, 3)
 HID_PIECES = ((32, 32, 64), (64, 64))
 
@@ -84,8 +84,8 @@ def tile_list_boundedgaps_lagged_rowabove_kernel(tc, xa, xb, hb, fk, w, wb_words
         cap_row(2)
         cap_row(3)
         w_bf = sbuf("w_bf", [P, PACK * R], BF16)
-        w_dst = w_bf[:].rearrange("p (s m t) -> p m t s", s=PACK, t=PACK)
-        w_src = w_raw[:].rearrange("p t (m s) -> p m t s", s=PACK)
+        w_dst = w_bf[:].rearrange("p (s m t) -> p m s t", s=PACK, t=PACK)
+        w_src = w_raw[:].rearrange("p t (m s) -> p m s t", s=PACK)
         nc.vector.tensor_copy(w_dst[:, 0:W_SPLIT], w_src[:, 0:W_SPLIT])
         nc.scalar.copy(w_dst[:, W_SPLIT:P], w_src[:, W_SPLIT:P])
         w_codes = sbuf("w_codes", [P, R], U32)

@@ -24,7 +24,7 @@ QUARTER = J // 4
 LAG = 2
 W_SPLIT = 80
 ROW_ORDER = (2, 0, 1, 3)
-HID_PIECES = ((32, 32, 64), (64, 64))
+HID_PIECES = ((64, 64), (64, 64))
 
 
 def tile_list_boundedgaps_lagged_rowabove_kernel(tc, xa, xb, hb, fk, w, wb_words, wb_scales, rs, offs, offs2, out):
@@ -48,8 +48,6 @@ def tile_list_boundedgaps_lagged_rowabove_kernel(tc, xa, xb, hb, fk, w, wb_words
         resid = sbuf("resid", [P, 2, N], F32)
         relu_a = sbuf("relu_a", [P, PACK * (LAG + J)], F32)
 
-        taken_off = sbuf("taken_off", [P, N], F32)
-
         nc.gpsimd.memset(wb_scale[:].bitcast(I32), 0)
         nc.gpsimd.memset(relu_a[:, 0 : PACK * LAG], 0.0)
 
@@ -64,10 +62,10 @@ def tile_list_boundedgaps_lagged_rowabove_kernel(tc, xa, xb, hb, fk, w, wb_words
         nc.sync.dma_start(list_a[:], offs)
         for t in ROW_ORDER:
             nc.sync.dma_start(xa_rows[t][:], xa_v[:, t, :])
+        nc.sync.dma_start(resid[:], rs.rearrange("(h p) n -> p h n", p=P))
         nc.sync.dma_start(wb_codes[:], wb_words[0])
         for q in range(4):
             nc.sync.dma_start(wb_scale[32 * q : 32 * q + 4, :].bitcast(I32), wb_scales[0, 4 * q : 4 * q + 4, :].bitcast(I32))
-        nc.sync.dma_start(resid[:], rs.rearrange("(h p) n -> p h n", p=P))
 
         capped = {}
 
@@ -104,7 +102,7 @@ def tile_list_boundedgaps_lagged_rowabove_kernel(tc, xa, xb, hb, fk, w, wb_words
             else:
                 nc.vector.tensor_scalar(dst, src, factor[:, t : t + 1], None, ALU.mult)
 
-        pieces = {2: ((0, J),), 0: ((0, J),), 1: ((0, HALF), (HALF, HALF)), 3: ((0, QUARTER), (QUARTER, QUARTER), (HALF, HALF))}
+        pieces = {2: ((0, J),), 0: ((0, J),), 1: ((0, HALF), (HALF, HALF)), 3: ((0, HALF), (HALF, HALF))}
         for t in ROW_ORDER:
             gaps = []
             for lo, n in pieces[t]:
@@ -116,7 +114,7 @@ def tile_list_boundedgaps_lagged_rowabove_kernel(tc, xa, xb, hb, fk, w, wb_words
             for gap, lo, n in gaps:
                 for j in range(lo, lo + n, HALF):
                     h, m = j // HALF, min(n, HALF)
-                    scale_into(t >= 2 or h == 1, u_bf[h][:, j % HALF : j % HALF + m, t], gap[:, j - lo : j - lo + m], t)
+                    scale_into(t < 2, u_bf[h][:, j % HALF : j % HALF + m, t], gap[:, j - lo : j - lo + m], t)
         a_banks = []
         for h in range(2):
             u_codes = sbuf(f"u_codes{h}", [P, HALF], U32)
@@ -135,6 +133,11 @@ def tile_list_boundedgaps_lagged_rowabove_kernel(tc, xa, xb, hb, fk, w, wb_words
                 )
             a_banks.append(bank)
 
+        floor = sbuf("floor", [P, 2, N], F32)
+        nc.scalar.activation(floor[:], resid[:], ACT.Copy, scale=-0.3)
+        shifted = [sbuf(f"shifted{h}", [P, N], F32) for h in range(2)]
+        magnitude = sbuf("magnitude", [P, N], F32)
+        means = []
         for h in range(2):
             hid_bf = sbuf(f"hid_bf{h}", [P, PACK * HALF], BF16)
             j0 = 0
@@ -153,27 +156,23 @@ def tile_list_boundedgaps_lagged_rowabove_kernel(tc, xa, xb, hb, fk, w, wb_words
             hid_codes = sbuf(f"hid_codes{h}", [P, HALF], U32)
             hid_scale = sbuf(f"hid_scale{h}", [P, HALF], U8)
             nc.vector.quantize_mx(hid_codes[:].bitcast(E5M2), hid_scale[:], hid_bf[:])
-            prod = psum.tile([P, N], F32, name=f"p_bank{h}")
-            nc.tensor.matmul_mx(
-                out=prod[:],
-                lhsT=hid_codes[:].bitcast(E5M2),
-                lhsT_scale=hid_scale[:],
-                rhs=wb_codes[:].bitcast(E2M1),
-                rhs_scale=wb_scale[:],
-                start=True,
-                stop=True,
-            )
-            magnitude = sbuf(f"magnitude{h}", [P, N], F32)
+            banks = [psum.tile([P, N], F32, name=f"p_bank{h}_{b}") for b in range(1 + h)]
+            for bank in banks:
+                nc.tensor.matmul_mx(
+                    out=bank[:],
+                    lhsT=hid_codes[:].bitcast(E5M2),
+                    lhsT_scale=hid_scale[:],
+                    rhs=wb_codes[:].bitcast(E2M1),
+                    rhs_scale=wb_scale[:],
+                    start=True,
+                    stop=True,
+                )
+            nc.vector.tensor_tensor(shifted[h][:], banks[0][:], floor[:, h, :], ALU.add)
             mean = sbuf(f"mean{h}", [P, 1], F32)
-            nc.scalar.activation(magnitude[:], prod[:], ACT.Abs, scale=1.0 / N, accum_out=mean[:])
-            parts = 1 + h
-            part = N // parts
-            offsets_n = [slice(c * part, (c + 1) * part) for c in range(parts)]
-            off = [taken_off[:, offsets_n[c]] for c in range(parts)]
-            y = [sbuf(f"y{h}_{c}", [P, part], F32) for c in range(parts)]
-            for c in range(parts):
-                nc.vector.tensor_scalar(off[c], resid[:, h, offsets_n[c]], 0.3, mean[:], ALU.mult, ALU.add)
-            for c in range(parts):
-                nc.vector.scalar_tensor_tensor(y[c][:], prod[:, offsets_n[c]], mean[:], off[c], ALU.max, ALU.subtract)
-                queue = nc.sync if c == parts - 1 else nc.scalar
-                queue.dma_start(out[halves[h], offsets_n[c]], y[c][:])
+            nc.scalar.activation(magnitude[:], banks[h][:], ACT.Abs, scale=1.0 / N, accum_out=mean[:])
+            means.append(mean)
+
+        for h in range(2):
+            y = sbuf(f"y{h}", [P, N], F32)
+            nc.vector.scalar_tensor_tensor(y[:], shifted[h][:], means[h][:], floor[:, h, :], ALU.subtract, ALU.max)
+            nc.sync.dma_start(out[halves[h], :], y[:])

from contextlib import ExitStack

import concourse.mybir as mybir

K, T, J, S, R, N = 512, 1024, 256, 512, 512, 256
FLOPS = 2 * K * R * J + 2 * R * J * N

F32 = mybir.dt.float32
BF16 = mybir.dt.bfloat16
I32 = mybir.dt.int32
U32 = mybir.dt.uint32
U16 = mybir.dt.uint16
U8 = mybir.dt.uint8
E4M3 = mybir.dt.float8_e4m3fn_x4
E5M2 = mybir.dt.float8_e5m2_x4
E2M1 = mybir.dt.float4_e2m1fn_x4
ALU = mybir.AluOpType
ACT = mybir.ActivationFunctionType

P = 128
PACK = 4
HALF = J // 2
QUARTER = J // 4
LAG = 2
W_SPLIT = 80
ROW_ORDER = (2, 0, 1, 3)
HID_PIECES = ((64, 64), (64, 64))


def tile_list_boundedgaps_lagged_rowabove_kernel(tc, xa, xb, hb, fk, w, wb_words, wb_scales, rs, offs, offs2, out):
    nc = tc.nc
    with ExitStack() as ctx:
        keep = ctx.enter_context(tc.tile_pool(name="keep", bufs=1))
        psum = ctx.enter_context(tc.psum_pool(name="psum", bufs=1))

        def sbuf(name, shape, dtype):
            return keep.tile(shape, dtype, name=name, align_bytes=64)

        list_a = sbuf("list_a", [P, J // 16], U16)
        list_b = sbuf("list_b", [P, J // 16], U16)
        w_raw = sbuf("w_raw", [P, PACK, R], F32)
        bound = sbuf("bound", [P, PACK], F32)
        factor = sbuf("factor", [P, PACK], F32)
        xb_pairs = [sbuf(f"xb_pair{i}", [P, 2, S], F32) for i in range(2)]
        xa_rows = [sbuf(f"xa_row{t}", [P, T], F32) for t in range(PACK)]
        wb_codes = sbuf("wb_codes", [P, 2 * N], U8)
        wb_scale = sbuf("wb_scale", [P, N], U8)
        resid = sbuf("resid", [P, 2, N], F32)
        relu_a = sbuf("relu_a", [P, PACK * (LAG + J)], F32)

        nc.gpsimd.memset(wb_scale[:].bitcast(I32), 0)
        nc.gpsimd.memset(relu_a[:, 0 : PACK * LAG], 0.0)

        xa_v = xa.rearrange("(p t) c -> p t c", t=PACK)
        xb_v = xb.rearrange("(p t) c -> p t c", t=PACK)
        nc.scalar.dma_start(bound[:], hb.rearrange("(p t) o -> p (t o)", t=PACK))
        nc.scalar.dma_start(factor[:], fk.rearrange("(p t) o -> p (t o)", t=PACK))
        nc.sync.dma_start(xb_pairs[1][:], xb_v[:, 2:4, :])
        nc.sync.dma_start(list_b[:], offs2)
        nc.sync.dma_start(w_raw[:], w.rearrange("(p t) r -> p t r", t=PACK))
        nc.sync.dma_start(xb_pairs[0][:], xb_v[:, 0:2, :])
        nc.sync.dma_start(list_a[:], offs)
        for t in ROW_ORDER:
            nc.sync.dma_start(xa_rows[t][:], xa_v[:, t, :])
        nc.sync.dma_start(resid[:], rs.rearrange("(h p) n -> p h n", p=P))
        nc.sync.dma_start(wb_codes[:], wb_words[0])
        for q in range(4):
            nc.sync.dma_start(wb_scale[32 * q : 32 * q + 4, :].bitcast(I32), wb_scales[0, 4 * q : 4 * q + 4, :].bitcast(I32))

        capped = {}

        def cap_row(t):
            picked_b = sbuf(f"picked_b{t}", [P, J], F32)
            window = xb_pairs[t // 2][:, t % 2, :].indirect(list_b[:])
            if t >= 2:
                nc.vector.tensor_copy(picked_b[:], window)
            else:
                nc.scalar.activation(picked_b[:], window, ACT.Copy)
            capped[t] = sbuf(f"capped{t}", [P, J], F32)
            nc.vector.tensor_scalar(capped[t][:], picked_b[:], bound[:, t : t + 1], None, ALU.min)

        cap_row(2)
        cap_row(3)
        w_bf = sbuf("w_bf", [P, PACK * R], BF16)
        w_dst = w_bf[:].rearrange("p (s m t) -> p m s t", s=PACK, t=PACK)
        w_src = w_raw[:].rearrange("p t (m s) -> p m s t", s=PACK)
        nc.vector.tensor_copy(w_dst[:, 0:W_SPLIT], w_src[:, 0:W_SPLIT])
        nc.scalar.copy(w_dst[:, W_SPLIT:P], w_src[:, W_SPLIT:P])
        w_codes = sbuf("w_codes", [P, R], U32)
        w_scale = sbuf("w_scale", [P, R], U8)
        nc.vector.quantize_mx(w_codes[:].bitcast(E5M2), w_scale[:], w_bf[:])

        cap_row(0)
        cap_row(1)

        u_bf = [sbuf(f"u_bf{h}", [P, HALF, PACK], BF16) for h in range(2)]
        halves = [slice(h * HALF, (h + 1) * HALF) for h in range(2)]

        def scale_into(on_scalar, dst, src, t):
            if on_scalar:
                nc.scalar.activation(dst, src, ACT.Copy, scale=factor[:, t : t + 1])
            else:
                nc.vector.tensor_scalar(dst, src, factor[:, t : t + 1], None, ALU.mult)

        pieces = {2: ((0, J),), 0: ((0, J),), 1: ((0, HALF), (HALF, HALF)), 3: ((0, HALF), (HALF, HALF))}
        for t in ROW_ORDER:
            gaps = []
            for lo, n in pieces[t]:
                gap = sbuf(f"gap{t}_{lo}", [P, n], F32)
                nc.vector.tensor_tensor(
                    gap[:], xa_rows[t][:].indirect(list_a[:, lo // 16 : (lo + n) // 16]), capped[t][:, lo : lo + n], ALU.subtract
                )
                gaps.append((gap, lo, n))
            for gap, lo, n in gaps:
                for j in range(lo, lo + n, HALF):
                    h, m = j // HALF, min(n, HALF)
                    scale_into(t < 2, u_bf[h][:, j % HALF : j % HALF + m, t], gap[:, j - lo : j - lo + m], t)
        a_banks = []
        for h in range(2):
            u_codes = sbuf(f"u_codes{h}", [P, HALF], U32)
            u_scale = sbuf(f"u_scale{h}", [P, HALF], U8)
            nc.vector.quantize_mx(u_codes[:].bitcast(E4M3), u_scale[:], u_bf[h][:].rearrange("p j t -> p (j t)"))
            bank = psum.tile([P, PACK, HALF], F32, name=f"a_bank{h}")
            for s in range(PACK):
                nc.tensor.matmul_mx(
                    out=bank[:, s, :],
                    lhsT=w_codes[:, s * P : (s + 1) * P].bitcast(E5M2),
                    lhsT_scale=w_scale[:, s * P : (s + 1) * P],
                    rhs=u_codes[:].bitcast(E4M3),
                    rhs_scale=u_scale[:],
                    start=True,
                    stop=True,
                )
            a_banks.append(bank)

        floor = sbuf("floor", [P, 2, N], F32)
        nc.scalar.activation(floor[:], resid[:], ACT.Copy, scale=-0.3)
        shifted = [sbuf(f"shifted{h}", [P, N], F32) for h in range(2)]
        magnitude = sbuf("magnitude", [P, N], F32)
        means = []
        for h in range(2):
            hid_bf = sbuf(f"hid_bf{h}", [P, PACK * HALF], BF16)
            j0 = 0
            for n in HID_PIECES[h]:
                lo, width = PACK * (h * HALF + j0), PACK * n
                now = relu_a[:, PACK * LAG + lo : PACK * LAG + lo + width]
                nc.scalar.activation(
                    now.rearrange("p (j s) -> p j s", s=PACK),
                    a_banks[h][:, :, j0 : j0 + n].rearrange("p s j -> p j s"),
                    ACT.Relu,
                )
                nc.vector.scalar_tensor_tensor(
                    hid_bf[:, PACK * j0 : PACK * j0 + width], relu_a[:, lo : lo + width], -0.5, now, ALU.mult, ALU.add
                )
                j0 = j0 + n
            hid_codes = sbuf(f"hid_codes{h}", [P, HALF], U32)
            hid_scale = sbuf(f"hid_scale{h}", [P, HALF], U8)
            nc.vector.quantize_mx(hid_codes[:].bitcast(E5M2), hid_scale[:], hid_bf[:])
            banks = [psum.tile([P, N], F32, name=f"p_bank{h}_{b}") for b in range(1 + h)]
            for bank in banks:
                nc.tensor.matmul_mx(
                    out=bank[:],
                    lhsT=hid_codes[:].bitcast(E5M2),
                    lhsT_scale=hid_scale[:],
                    rhs=wb_codes[:].bitcast(E2M1),
                    rhs_scale=wb_scale[:],
                    start=True,
                    stop=True,
                )
            nc.vector.tensor_tensor(shifted[h][:], banks[0][:], floor[:, h, :], ALU.add)
            mean = sbuf(f"mean{h}", [P, 1], F32)
            nc.scalar.activation(magnitude[:], banks[h][:], ACT.Abs, scale=1.0 / N, accum_out=mean[:])
            means.append(mean)

        for h in range(2):
            y = sbuf(f"y{h}", [P, N], F32)
            nc.vector.scalar_tensor_tensor(y[:], shifted[h][:], means[h][:], floor[:, h, :], ALU.subtract, ALU.max)
            nc.sync.dma_start(out[halves[h], :], y[:])
